import numpy as np
import ml_dtypes


def mxq(x, axis, fmt="e4m3"):
    dtype, down = {"e4m3": (ml_dtypes.float8_e4m3fn, 7), "e5m2": (ml_dtypes.float8_e5m2, 14)}[fmt]
    v = np.moveaxis(np.asarray(x, np.float32).astype(ml_dtypes.bfloat16).astype(np.float64), axis, -1)
    blocks = v.reshape(v.shape[:-1] + (-1, 32))
    amax = np.abs(blocks).max(-1, keepdims=True)
    byte = np.maximum(np.where(amax > 0, np.frexp(amax)[1] - 1 + 127, 0) - down, 1)
    scale = np.exp2(byte - 127.0)
    codes = (blocks / scale).astype(np.float32).astype(dtype).astype(np.float64)
    return np.moveaxis((codes * scale).reshape(v.shape), -1, axis)


WIDE = False


def mx_kscale(k):
    if not WIDE:
        return np.ones(k)
    levels = np.array([30, -30])
    if k % 512:
        return np.exp2(np.random.permutation(np.resize(levels, k // 32))).repeat(32)
    a = np.empty((k // 512, 16))
    for p in range(k // 512):
        a[p, :8] = np.random.permutation(np.resize(levels, 8))
        for g in range(8):
            far = levels[np.abs(levels - a[p, g]) >= 10]
            a[p, g + 8] = far[np.random.randint(len(far))]
    return np.exp2(a.ravel()).repeat(32)


def f64(x):
    return np.asarray(x).astype(np.float64)


def striped(idx):
    return np.tile(np.asarray(idx).reshape(-1, 16).T, (8, 1)).astype(np.uint16)


def unstriped(offs):
    return offs[:16].T.reshape(-1).astype(np.int64)


K, J, N, T, V, E = 256, 1024, 256, 2048, 2048, 128


def setup_inputs():
    n = np.random.standard_normal
    idx = np.random.permutation(T)[:J]
    idx2 = np.random.permutation(V)[:J]
    idx3 = np.random.permutation(N)[:E]
    fj = mx_kscale(J)
    return {
        "xf": (n((K, T))).astype(np.float32),
        "ra": (np.random.uniform(0.5, 1.5, (1, J)) * fj).astype(np.float32),
        "gt": (n((N, V)) * np.exp(0.5 * n((1, V)))).astype(np.float32),
        "rb": (np.random.uniform(0.5, 1.5, (1, J)) / fj).astype(np.float32),
        "cp": (np.random.uniform(0.4, 1.2, (N, 1))).astype(np.float32),
        "old": (0.5 * n((K, E))).astype(np.float32),
        "offs": striped(idx),
        "offs2": striped(idx2),
        "offs3": striped(idx3),
    }


def reference(xf, ra, gt, rb, cp, old, offs, offs2, offs3):
    idx = unstriped(offs)
    idx2 = unstriped(offs2)
    idx3 = unstriped(offs3)
    xg = f64(xf)[:, idx]
    x1 = np.pad(xg, ((0, 0), (1, 0)))[:, :J]
    us = (xg - 0.6 * x1) * f64(ra)
    uj = us.T
    gs = np.minimum(f64(gt)[:, idx2], f64(cp)) * f64(rb)
    gj = gs.T
    ujq = mxq(uj, 0, "e4m3")
    gjq = mxq(gj, 0, "e5m2")
    w = ujq.T @ gjq
    y = 0.04 * w[:, idx3] + f64(old)
    return y

@@ -1,0 +1,210 @@
+from contextlib import ExitStack
+
+import concourse.mybir as mybir
+from concourse.masks import make_identity
+
+K, J, N, T, V, E = 256, 1024, 256, 2048, 2048, 128
+FLOPS = 2 * K * N * J
+
+F32 = mybir.dt.float32
+BF16 = mybir.dt.bfloat16
+U32 = mybir.dt.uint32
+U16 = mybir.dt.uint16
+U8 = mybir.dt.uint8
+E4M3X4 = mybir.dt.float8_e4m3fn_x4
+E5M2X4 = mybir.dt.float8_e5m2_x4
+ALU = mybir.AluOpType
+COPY = mybir.ActivationFunctionType.Copy
+
+P = 128
+PACK = 4
+J_PASS = P * PACK
+PASSES = J // J_PASS
+LEAD = 8
+PER_COL = 16
+
+
+def tile_list_moment_steps_bounded_columns_kernel(tc, xf, ra, gt, rb, cp, old, offs, offs2, offs3, out):
+    nc = tc.nc
+    with ExitStack() as ctx:
+        held = ctx.enter_context(tc.tile_pool(name="held", bufs=1))
+        psum = ctx.enter_context(tc.psum_pool(name="psum", bufs=1))
+
+        list_x = held.tile([P, J // PER_COL], U16, name="list_x")
+        list_g = held.tile([P, J // PER_COL], U16, name="list_g")
+        list_w = held.tile([P, E // PER_COL], U16, name="list_w")
+        x_table = [held.tile([P, T], F32, name=f"x_table{i}") for i in range(2)]
+        g_table = [held.tile([P, V], F32, name=f"g_table{i}") for i in range(2)]
+        ra_sb = held.tile([P, PASSES, PACK], F32, name="ra_sb")
+        rb_sb = held.tile([P, PASSES, PACK], F32, name="rb_sb")
+        cp_sb = held.tile([P, 2], F32, name="cp_sb")
+        old_sb = held.tile([P, 2 * E], F32, name="old_sb")
+        ident = held.tile([P, P], F32, name="ident")
+
+        xf_rows = xf.rearrange("(p i) c -> i p c", i=2)
+        nc.sync.dma_start(list_x[:], offs)
+        nc.sync.dma_start(x_table[0][:], xf_rows[0])
+        nc.scalar.dma_start(rb_sb[:], rb.rearrange("o (a p t) -> p (o a) t", a=PASSES, t=PACK))
+        nc.scalar.dma_start(ra_sb[:], ra.rearrange("o (a p t) -> p (o a) t", a=PASSES, t=PACK))
+        with nc.allow_non_contiguous_dma(reason="one bound a partition"):
+            nc.scalar.dma_start(cp_sb[:], cp.rearrange("(i p) o -> p (i o)", p=P))
+        nc.sync.dma_start(x_table[1][:], xf_rows[1])
+        nc.sync.dma_start(list_g[:], offs2)
+        nc.sync.dma_start(g_table[0][:], gt[0:P, :])
+        nc.sync.dma_start(g_table[1][:], gt[P : 2 * P, :])
+        nc.sync.dma_start(list_w[:], offs3)
+        nc.sync.dma_start(old_sb[:], old.rearrange("(p i) e -> p (i e)", i=2))
+
+        make_identity(nc, ident[:])
+
+        x_picked = [held.tile([P, LEAD + J], F32, name=f"x_picked{i}") for i in range(2)]
+        g_picked = [held.tile([P, J], F32, name=f"g_picked{i}") for i in range(2)]
+        for i in range(2):
+            nc.gpsimd.memset(x_picked[i][:, 0:LEAD], 0.0)
+
+        rb_rows = [psum.tile([P, PACK, P], F32, name=f"rb_rows{a}") for a in range(PASSES)]
+        for a in range(PASSES):
+            for t in range(PACK):
+                nc.tensor.transpose(rb_rows[a][:, t, :], rb_sb[:, a, t : t + 1].to_broadcast([P, P]), ident[:])
+
+        x_codes = [held.tile([P, PASSES, P], U32, name=f"x_codes{i}", align_bytes=64) for i in range(2)]
+        x_scales = [held.tile([P, PASSES, P], U8, name=f"x_scales{i}", align_bytes=64) for i in range(2)]
+        g_codes = [held.tile([P, PASSES, P], U32, name=f"g_codes{i}", align_bytes=64) for i in range(2)]
+        g_scales = [held.tile([P, PASSES, P], U8, name=f"g_scales{i}", align_bytes=64) for i in range(2)]
+        x_diff = [[held.tile([P, J_PASS], F32, name=f"x_diff{i}{a}") for a in range(PASSES)] for i in range(2)]
+        x_grouped = [held.tile([P, PASSES, P, PACK], BF16, name=f"x_grouped{i}", align_bytes=64) for i in range(2)]
+        g_rounded = [[held.tile([P, J_PASS], BF16, name=f"g_rounded{i}{a}") for a in range(PASSES)] for i in range(2)]
+        g_grouped = [
+            [held.tile([P, P, PACK], BF16, name=f"g_grouped{i}{a}", align_bytes=64) for a in range(PASSES)]
+            for i in range(2)
+        ]
+        w_sb = [held.tile([P, N], F32, name=f"w_sb{i}") for i in range(2)]
+        w_picked = held.tile([P, 2 * E], F32, name="w_picked")
+        result = held.tile([P, 2 * E], F32, name="result")
+        turned = {}
+
+        def gather(engine, dst, table, entries, j0, j1):
+            src = table[:].indirect(entries[:, j0 // PER_COL : j1 // PER_COL])
+            if engine == "vector":
+                nc.vector.tensor_copy(dst, src)
+            else:
+                nc.scalar.activation(dst, src, COPY)
+
+        def gather_x(engine, i, j0, j1):
+            gather(engine, x_picked[i][:, LEAD + j0 : LEAD + j1], x_table[i], list_x, j0, j1)
+
+        def gather_g(engine, i, j0, j1):
+            gather(engine, g_picked[i][:, j0:j1], g_table[i], list_g, j0, j1)
+
+        def diff_x(i, a):
+            j0 = LEAD + a * J_PASS
+            nc.vector.scalar_tensor_tensor(
+                x_diff[i][a][:], x_picked[i][:, j0 - 1 : j0 - 1 + J_PASS], -0.6,
+                x_picked[i][:, j0 : j0 + J_PASS], ALU.mult, ALU.add,
+            )
+            bank = psum.tile([P, PACK, P], F32, name="bank", tag="turn", bufs=4)
+            for t in range(PACK):
+                nc.tensor.transpose(bank[:, t, :], x_diff[i][a][:, t:J_PASS:PACK], ident[:])
+            turned["x", i, a] = bank
+
+        def weigh_x(i, a):
+            nc.vector.tensor_tensor(
+                x_grouped[i][:, a, :, :],
+                turned["x", i, a][:].rearrange("p t k -> p k t"),
+                ra_sb[:, a, :].unsqueeze(1).to_broadcast([P, P, PACK]),
+                ALU.mult,
+            )
+
+        def quantize_x(i):
+            nc.vector.quantize_mx(
+                out=x_codes[i][:].rearrange("p a k -> p (a k)").bitcast(E4M3X4),
+                scales=x_scales[i][:].rearrange("p a k -> p (a k)"),
+                in_=x_grouped[i][:].rearrange("p a k t -> p (a k t)"),
+            )
+
+        def bound_g(i, a):
+            j0 = a * J_PASS
+            nc.vector.scalar_tensor_tensor(
+                g_rounded[i][a][:].rearrange("p (q t) -> p q t", t=PACK),
+                g_picked[i][:, j0 : j0 + J_PASS].rearrange("p (q t) -> p q t", t=PACK),
+                cp_sb[:, i : i + 1],
+                rb_rows[a][:].rearrange("p t q -> p q t"),
+                ALU.min, ALU.mult,
+            )
+            bank = psum.tile([P, PACK, P], F32, name="bank", tag="turn", bufs=4)
+            words = g_rounded[i][a][:].bitcast(F32)
+            for u in range(2):
+                nc.tensor.transpose(bank[:, u, :], words[:, u : J_PASS // 2 : 2], ident[:])
+            turned["g", i, a] = bank
+
+        def group_g(i, a):
+            nc.scalar.copy(
+                g_grouped[i][a][:].rearrange("p n t -> p (n t)").bitcast(F32).rearrange("p (n u) -> p n u", u=2),
+                turned["g", i, a][:, 0:2, :].rearrange("p u n -> p n u"),
+            )
+
+        def quantize_g(i, a):
+            nc.vector.quantize_mx(
+                out=g_codes[i][:, a, :].bitcast(E5M2X4),
+                scales=g_scales[i][:, a, :],
+                in_=g_grouped[i][a][:].rearrange("p n t -> p (n t)"),
+            )
+
+        def multiply(acc, i, h, a):
+            nc.tensor.matmul_mx(
+                out=acc[:],
+                lhsT=x_codes[i][:, a, :].bitcast(E4M3X4),
+                lhsT_scale=x_scales[i][:, a, :],
+                rhs=g_codes[h][:, a, :].bitcast(E5M2X4),
+                rhs_scale=g_scales[h][:, a, :],
+                start=(a == 0),
+                stop=(a == PASSES - 1),
+            )
+
+        def moments(h):
+            accs = [psum.tile([P, P], F32, name="acc", tag=f"acc{i}") for i in range(2)]
+            for a in range(PASSES):
+                for i in range(2):
+                    multiply(accs[i], i, h, a)
+            nc.vector.tensor_copy(w_sb[0][:, h * P : (h + 1) * P], accs[0][:])
+            nc.scalar.copy(w_sb[1][:, h * P : (h + 1) * P], accs[1][:])
+
+        gather_x("vector", 0, 0, 512)
+        gather_x("scalar", 0, 512, 1024)
+        diff_x(0, 0)
+        diff_x(0, 1)
+        weigh_x(0, 0)
+        gather_x("scalar", 1, 0, 512)
+        gather_x("vector", 1, 768, 1024)
+        gather_x("scalar", 1, 512, 768)
+        weigh_x(0, 1)
+        diff_x(1, 0)
+        quantize_x(0)
+        diff_x(1, 1)
+        gather_g("scalar", 0, 0, 512)
+        gather_g("scalar", 0, 512, 1024)
+        weigh_x(1, 0)
+        bound_g(0, 0)
+        weigh_x(1, 1)
+        group_g(0, 0)
+        bound_g(0, 1)
+        quantize_x(1)
+        gather_g("scalar", 1, 0, 512)
+        group_g(0, 1)
+        quantize_g(0, 0)
+        gather_g("scalar", 1, 512, 768)
+        gather_g("vector", 1, 768, 1024)
+        quantize_g(0, 1)
+        bound_g(1, 0)
+        group_g(1, 0)
+        bound_g(1, 1)
+        moments(0)
+        quantize_g(1, 0)
+        group_g(1, 1)
+        quantize_g(1, 1)
+        moments(1)
+
+        nc.vector.tensor_copy(w_picked[:, 0:E], w_sb[0][:].indirect(list_w[:]))
+        nc.scalar.activation(w_picked[:, E : 2 * E], w_sb[1][:].indirect(list_w[:]), COPY)
+        nc.vector.scalar_tensor_tensor(result[:], w_picked[:], 0.04, old_sb[:], ALU.mult, ALU.add)
+        nc.sync.dma_start(out.rearrange("(p i) e -> p (i e)", i=2), result[:])

@@ -45,39 +45,39 @@ def tile_list_moment_steps_bounded_columns_kernel(tc, xf, ra, gt, rb, cp, old, o
         nc.sync.dma_start(list_x[:], offs)
         nc.sync.dma_start(x_table[0][:], xf_rows[0])
         nc.scalar.dma_start(rb_sb[:], rb.rearrange("o (a p t) -> p (o a) t", a=PASSES, t=PACK))
-        nc.scalar.dma_start(ra_sb[:], ra.rearrange("o (a p t) -> p (o a) t", a=PASSES, t=PACK))
         with nc.allow_non_contiguous_dma(reason="one bound a partition"):
             nc.scalar.dma_start(cp_sb[:], cp.rearrange("(i p) o -> p (i o)", p=P))
         nc.sync.dma_start(x_table[1][:], xf_rows[1])
+        nc.sync.dma_start(ra_sb[:], ra.rearrange("o (a p t) -> p (o a) t", a=PASSES, t=PACK))
         nc.sync.dma_start(list_g[:], offs2)
         nc.sync.dma_start(g_table[0][:], gt[0:P, :])
         nc.sync.dma_start(g_table[1][:], gt[P : 2 * P, :])
         nc.sync.dma_start(list_w[:], offs3)
         nc.sync.dma_start(old_sb[:], old.rearrange("(p i) e -> p (i e)", i=2))
 
-        make_identity(nc, ident[:])
-
         x_picked = [held.tile([P, LEAD + J], F32, name=f"x_picked{i}") for i in range(2)]
-        g_picked = [held.tile([P, J], F32, name=f"g_picked{i}") for i in range(2)]
-        for i in range(2):
-            nc.gpsimd.memset(x_picked[i][:, 0:LEAD], 0.0)
+        g_picked = [
+            [held.tile([P, J_PASS], F32, name=f"g_picked{i}{a}", align_bytes=64) for a in range(PASSES)]
+            for i in range(2)
+        ]
+        nc.vector.memset(x_picked[1][:, 0:LEAD], 0.0)
+        nc.scalar.activation(x_picked[0][:, 0:LEAD], x_picked[1][:, 0:LEAD], COPY)
+
+        make_identity(nc, ident[:])
 
         rb_rows = [psum.tile([P, PACK, P], F32, name=f"rb_rows{a}") for a in range(PASSES)]
         for a in range(PASSES):
             for t in range(PACK):
                 nc.tensor.transpose(rb_rows[a][:, t, :], rb_sb[:, a, t : t + 1].to_broadcast([P, P]), ident[:])
 
-        x_codes = [held.tile([P, PASSES, P], U32, name=f"x_codes{i}", align_bytes=64) for i in range(2)]
+        x_codes = {}
         x_scales = [held.tile([P, PASSES, P], U8, name=f"x_scales{i}", align_bytes=64) for i in range(2)]
         g_codes = [held.tile([P, PASSES, P], U32, name=f"g_codes{i}", align_bytes=64) for i in range(2)]
         g_scales = [held.tile([P, PASSES, P], U8, name=f"g_scales{i}", align_bytes=64) for i in range(2)]
         x_diff = [[held.tile([P, J_PASS], F32, name=f"x_diff{i}{a}") for a in range(PASSES)] for i in range(2)]
-        x_grouped = [held.tile([P, PASSES, P, PACK], BF16, name=f"x_grouped{i}", align_bytes=64) for i in range(2)]
+        x_grouped = {0: held.tile([P, PASSES, P, PACK], BF16, name="x_grouped0", align_bytes=64)}
         g_rounded = [[held.tile([P, J_PASS], BF16, name=f"g_rounded{i}{a}") for a in range(PASSES)] for i in range(2)]
-        g_grouped = [
-            [held.tile([P, P, PACK], BF16, name=f"g_grouped{i}{a}", align_bytes=64) for a in range(PASSES)]
-            for i in range(2)
-        ]
+        g_grouped = {}
         w_sb = [held.tile([P, N], F32, name=f"w_sb{i}") for i in range(2)]
         w_picked = held.tile([P, 2 * E], F32, name="w_picked")
         result = held.tile([P, 2 * E], F32, name="result")
@@ -94,7 +94,8 @@ def tile_list_moment_steps_bounded_columns_kernel(tc, xf, ra, gt, rb, cp, old, o
             gather(engine, x_picked[i][:, LEAD + j0 : LEAD + j1], x_table[i], list_x, j0, j1)
 
         def gather_g(engine, i, j0, j1):
-            gather(engine, g_picked[i][:, j0:j1], g_table[i], list_g, j0, j1)
+            a = j0 // J_PASS
+            gather(engine, g_picked[i][a][:, j0 - a * J_PASS : j1 - a * J_PASS], g_table[i], list_g, j0, j1)
 
         def diff_x(i, a):
             j0 = LEAD + a * J_PASS
@@ -102,7 +103,7 @@ def tile_list_moment_steps_bounded_columns_kernel(tc, xf, ra, gt, rb, cp, old, o
                 x_diff[i][a][:], x_picked[i][:, j0 - 1 : j0 - 1 + J_PASS], -0.6,
                 x_picked[i][:, j0 : j0 + J_PASS], ALU.mult, ALU.add,
             )
-            bank = psum.tile([P, PACK, P], F32, name="bank", tag="turn", bufs=4)
+            bank = psum.tile([P, PACK, P], F32, name="bank", tag=f"turn{2 * i + a}")
             for t in range(PACK):
                 nc.tensor.transpose(bank[:, t, :], x_diff[i][a][:, t:J_PASS:PACK], ident[:])
             turned["x", i, a] = bank
@@ -117,21 +118,22 @@ def tile_list_moment_steps_bounded_columns_kernel(tc, xf, ra, gt, rb, cp, old, o
 
         def quantize_x(i):
             nc.vector.quantize_mx(
-                out=x_codes[i][:].rearrange("p a k -> p (a k)").bitcast(E4M3X4),
+                out=x_codes[i].rearrange("p a k -> p (a k)").bitcast(E4M3X4),
                 scales=x_scales[i][:].rearrange("p a k -> p (a k)"),
                 in_=x_grouped[i][:].rearrange("p a k t -> p (a k t)"),
             )
 
-        def bound_g(i, a):
-            j0 = a * J_PASS
+        def bound_g(i, a, q0=0, q1=P):
             nc.vector.scalar_tensor_tensor(
-                g_rounded[i][a][:].rearrange("p (q t) -> p q t", t=PACK),
-                g_picked[i][:, j0 : j0 + J_PASS].rearrange("p (q t) -> p q t", t=PACK),
+                g_rounded[i][a][:].rearrange("p (q t) -> p q t", t=PACK)[:, q0:q1, :],
+                g_picked[i][a][:].rearrange("p (q t) -> p q t", t=PACK)[:, q0:q1, :],
                 cp_sb[:, i : i + 1],
-                rb_rows[a][:].rearrange("p t q -> p q t"),
+                rb_rows[a][:].rearrange("p t q -> p q t")[:, q0:q1, :],
                 ALU.min, ALU.mult,
             )
-            bank = psum.tile([P, PACK, P], F32, name="bank", tag="turn", bufs=4)
+
+        def turn_g(i, a):
+            bank = psum.tile([P, PACK, P], F32, name="bank", tag=f"turn{3 - 2 * i - a}")
             words = g_rounded[i][a][:].bitcast(F32)
             for u in range(2):
                 nc.tensor.transpose(bank[:, u, :], words[:, u : J_PASS // 2 : 2], ident[:])
@@ -139,16 +141,12 @@ def tile_list_moment_steps_bounded_columns_kernel(tc, xf, ra, gt, rb, cp, old, o
 
         def group_g(i, a):
             nc.scalar.copy(
-                g_grouped[i][a][:].rearrange("p n t -> p (n t)").bitcast(F32).rearrange("p (n u) -> p n u", u=2),
+                g_grouped[i, a].bitcast(F32).rearrange("p (n u) -> p n u", u=2),
                 turned["g", i, a][:, 0:2, :].rearrange("p u n -> p n u"),
             )
 
-        def quantize_g(i, a):
-            nc.vector.quantize_mx(
-                out=g_codes[i][:, a, :].bitcast(E5M2X4),
-                scales=g_scales[i][:, a, :],
-                in_=g_grouped[i][a][:].rearrange("p n t -> p (n t)"),
-            )
+        def quantize_g(codes, scales, grouped):
+            nc.vector.quantize_mx(out=codes.bitcast(E5M2X4), scales=scales, in_=grouped)
 
         def multiply(acc, i, h, a):
             nc.tensor.matmul_mx(
@@ -161,48 +159,63 @@ def tile_list_moment_steps_bounded_columns_kernel(tc, xf, ra, gt, rb, cp, old, o
                 stop=(a == PASSES - 1),
             )
 
-        def moments(h):
-            accs = [psum.tile([P, P], F32, name="acc", tag=f"acc{i}") for i in range(2)]
-            for a in range(PASSES):
-                for i in range(2):
-                    multiply(accs[i], i, h, a)
-            nc.vector.tensor_copy(w_sb[0][:, h * P : (h + 1) * P], accs[0][:])
-            nc.scalar.copy(w_sb[1][:, h * P : (h + 1) * P], accs[1][:])
+        accs = {}
+        for i in range(2):
+            accs[i, 0] = psum.tile([P, P], F32, name="acc", tag=f"acc{i}")
 
-        gather_x("vector", 0, 0, 512)
+        gather_x("vector", 0, 0, 256)
+        gather_x("scalar", 0, 256, 512)
         gather_x("scalar", 0, 512, 1024)
         diff_x(0, 0)
         diff_x(0, 1)
+        gather_x("vector", 1, 0, 256)
+        gather_x("scalar", 1, 256, 512)
+        gather_x("scalar", 1, 512, 1024)
         weigh_x(0, 0)
-        gather_x("scalar", 1, 0, 512)
-        gather_x("vector", 1, 768, 1024)
-        gather_x("scalar", 1, 512, 768)
-        weigh_x(0, 1)
         diff_x(1, 0)
-        quantize_x(0)
         diff_x(1, 1)
+        weigh_x(0, 1)
         gather_g("scalar", 0, 0, 512)
-        gather_g("scalar", 0, 512, 1024)
-        weigh_x(1, 0)
-        bound_g(0, 0)
-        weigh_x(1, 1)
-        group_g(0, 0)
-        bound_g(0, 1)
-        quantize_x(1)
+        gather_g("scalar", 0, 512, 768)
+        gather_g("vector", 0, 768, 1024)
         gather_g("scalar", 1, 0, 512)
-        group_g(0, 1)
-        quantize_g(0, 0)
         gather_g("scalar", 1, 512, 768)
-        gather_g("vector", 1, 768, 1024)
-        quantize_g(0, 1)
+        gather_g("scalar", 1, 768, 1024)
+        bound_g(0, 0)
+        bound_g(0, 1)
+        x_grouped[1] = held.tile([P, PASSES, P, PACK], BF16, name="x_grouped1", tag="g_picked00", align_bytes=64)
+        weigh_x(1, 0)
+        weigh_x(1, 1)
         bound_g(1, 0)
-        group_g(1, 0)
-        bound_g(1, 1)
-        moments(0)
-        quantize_g(1, 0)
-        group_g(1, 1)
-        quantize_g(1, 1)
-        moments(1)
+        bound_g(1, 1, 0, P // 2)
+        bound_g(1, 1, P // 2, P)
+        first = held.tile([P, J], BF16, name="g_grouped0", tag="g_picked10", align_bytes=64)
+        for a in range(PASSES):
+            g_grouped[0, a] = first[:, a * J_PASS : (a + 1) * J_PASS]
+            g_grouped[1, a] = held.tile([P, J_PASS], BF16, name=f"g_grouped1{a}", align_bytes=64)[:]
+        for i in range(2):
+            for a in range(PASSES):
+                turn_g(i, a)
+                group_g(i, a)
+        both = held.tile([P, 2, PASSES, P], U32, name="x_codes", tag="g_picked11", align_bytes=64)
+        for i in range(2):
+            x_codes[i] = both[:, i, :, :]
+            accs[i, 1] = psum.tile([P, P], F32, name="acc", tag=f"turn{3 - i}")
+        quantize_x(0)
+        quantize_g(g_codes[0][:].rearrange("p a n -> p (a n)"), g_scales[0][:].rearrange("p a n -> p (a n)"), first[:])
+        quantize_x(1)
+        for a in range(PASSES):
+            quantize_g(g_codes[1][:, a, :], g_scales[1][:, a, :], g_grouped[1, a])
+        for i in range(2):
+            for a in range(PASSES):
+                multiply(accs[i, 0], i, 0, a)
+        for a in range(PASSES):
+            for i in range(2):
+                multiply(accs[i, 1], i, 1, a)
+        for i in range(2):
+            nc.scalar.copy(w_sb[i][:, 0:P], accs[i, 0][:])
+        nc.vector.tensor_copy(w_sb[0][:, P : 2 * P], accs[0, 1][:])
+        nc.scalar.copy(w_sb[1][:, P : 2 * P], accs[1, 1][:])
 
         nc.vector.tensor_copy(w_picked[:, 0:E], w_sb[0][:].indirect(list_w[:]))
         nc.scalar.activation(w_picked[:, E : 2 * E], w_sb[1][:].indirect(list_w[:]), COPY)

from contextlib import ExitStack

import concourse.mybir as mybir
from concourse.masks import make_identity

K, J, N, T, V, E = 256, 1024, 256, 2048, 2048, 128
FLOPS = 2 * K * N * J

F32 = mybir.dt.float32
BF16 = mybir.dt.bfloat16
U32 = mybir.dt.uint32
U16 = mybir.dt.uint16
U8 = mybir.dt.uint8
E4M3X4 = mybir.dt.float8_e4m3fn_x4
E5M2X4 = mybir.dt.float8_e5m2_x4
ALU = mybir.AluOpType
COPY = mybir.ActivationFunctionType.Copy

P = 128
PACK = 4
J_PASS = P * PACK
PASSES = J // J_PASS
LEAD = 8
PER_COL = 16


def tile_list_moment_steps_bounded_columns_kernel(tc, xf, ra, gt, rb, cp, old, offs, offs2, offs3, out):
    nc = tc.nc
    with ExitStack() as ctx:
        held = ctx.enter_context(tc.tile_pool(name="held", bufs=1))
        psum = ctx.enter_context(tc.psum_pool(name="psum", bufs=1))

        list_x = held.tile([P, J // PER_COL], U16, name="list_x")
        list_g = held.tile([P, J // PER_COL], U16, name="list_g")
        list_w = held.tile([P, E // PER_COL], U16, name="list_w")
        x_table = [held.tile([P, T], F32, name=f"x_table{i}") for i in range(2)]
        g_table = [held.tile([P, V], F32, name=f"g_table{i}") for i in range(2)]
        ra_sb = held.tile([P, PASSES, PACK], F32, name="ra_sb")
        rb_sb = held.tile([P, PASSES, PACK], F32, name="rb_sb")
        cp_sb = held.tile([P, 2], F32, name="cp_sb")
        old_sb = held.tile([P, 2 * E], F32, name="old_sb")
        ident = held.tile([P, P], F32, name="ident")

        xf_rows = xf.rearrange("(p i) c -> i p c", i=2)
        nc.sync.dma_start(list_x[:], offs)
        nc.sync.dma_start(x_table[0][:], xf_rows[0])
        nc.scalar.dma_start(rb_sb[:], rb.rearrange("o (a p t) -> p (o a) t", a=PASSES, t=PACK))
        with nc.allow_non_contiguous_dma(reason="one bound a partition"):
            nc.scalar.dma_start(cp_sb[:], cp.rearrange("(i p) o -> p (i o)", p=P))
        nc.sync.dma_start(x_table[1][:], xf_rows[1])
        nc.sync.dma_start(ra_sb[:], ra.rearrange("o (a p t) -> p (o a) t", a=PASSES, t=PACK))
        nc.sync.dma_start(list_g[:], offs2)
        nc.sync.dma_start(g_table[0][:], gt[0:P, :])
        nc.sync.dma_start(g_table[1][:], gt[P : 2 * P, :])
        nc.sync.dma_start(list_w[:], offs3)
        nc.sync.dma_start(old_sb[:], old.rearrange("(p i) e -> p (i e)", i=2))

        x_picked = [held.tile([P, LEAD + J], F32, name=f"x_picked{i}") for i in range(2)]
        g_picked = [
            [held.tile([P, J_PASS], F32, name=f"g_picked{i}{a}", align_bytes=64) for a in range(PASSES)]
            for i in range(2)
        ]
        nc.vector.memset(x_picked[1][:, 0:LEAD], 0.0)
        nc.scalar.activation(x_picked[0][:, 0:LEAD], x_picked[1][:, 0:LEAD], COPY)

        make_identity(nc, ident[:])

        rb_rows = [psum.tile([P, PACK, P], F32, name=f"rb_rows{a}") for a in range(PASSES)]
        for a in range(PASSES):
            for t in range(PACK):
                nc.tensor.transpose(rb_rows[a][:, t, :], rb_sb[:, a, t : t + 1].to_broadcast([P, P]), ident[:])

        x_codes = {}
        x_scales = [held.tile([P, PASSES, P], U8, name=f"x_scales{i}", align_bytes=64) for i in range(2)]
        g_codes = [held.tile([P, PASSES, P], U32, name=f"g_codes{i}", align_bytes=64) for i in range(2)]
        g_scales = [held.tile([P, PASSES, P], U8, name=f"g_scales{i}", align_bytes=64) for i in range(2)]
        x_diff = [[held.tile([P, J_PASS], F32, name=f"x_diff{i}{a}") for a in range(PASSES)] for i in range(2)]
        x_grouped = {0: held.tile([P, PASSES, P, PACK], BF16, name="x_grouped0", align_bytes=64)}
        g_rounded = [[held.tile([P, J_PASS], BF16, name=f"g_rounded{i}{a}") for a in range(PASSES)] for i in range(2)]
        g_grouped = {}
        w_sb = [held.tile([P, N], F32, name=f"w_sb{i}") for i in range(2)]
        w_picked = held.tile([P, 2 * E], F32, name="w_picked")
        result = held.tile([P, 2 * E], F32, name="result")
        turned = {}

        def gather(engine, dst, table, entries, j0, j1):
            src = table[:].indirect(entries[:, j0 // PER_COL : j1 // PER_COL])
            if engine == "vector":
                nc.vector.tensor_copy(dst, src)
            else:
                nc.scalar.activation(dst, src, COPY)

        def gather_x(engine, i, j0, j1):
            gather(engine, x_picked[i][:, LEAD + j0 : LEAD + j1], x_table[i], list_x, j0, j1)

        def gather_g(engine, i, j0, j1):
            a = j0 // J_PASS
            gather(engine, g_picked[i][a][:, j0 - a * J_PASS : j1 - a * J_PASS], g_table[i], list_g, j0, j1)

        def diff_x(i, a):
            j0 = LEAD + a * J_PASS
            nc.vector.scalar_tensor_tensor(
                x_diff[i][a][:], x_picked[i][:, j0 - 1 : j0 - 1 + J_PASS], -0.6,
                x_picked[i][:, j0 : j0 + J_PASS], ALU.mult, ALU.add,
            )
            bank = psum.tile([P, PACK, P], F32, name="bank", tag=f"turn{2 * i + a}")
            for t in range(PACK):
                nc.tensor.transpose(bank[:, t, :], x_diff[i][a][:, t:J_PASS:PACK], ident[:])
            turned["x", i, a] = bank

        def weigh_x(i, a):
            nc.vector.tensor_tensor(
                x_grouped[i][:, a, :, :],
                turned["x", i, a][:].rearrange("p t k -> p k t"),
                ra_sb[:, a, :].unsqueeze(1).to_broadcast([P, P, PACK]),
                ALU.mult,
            )

        def quantize_x(i):
            nc.vector.quantize_mx(
                out=x_codes[i].rearrange("p a k -> p (a k)").bitcast(E4M3X4),
                scales=x_scales[i][:].rearrange("p a k -> p (a k)"),
                in_=x_grouped[i][:].rearrange("p a k t -> p (a k t)"),
            )

        def bound_g(i, a, q0=0, q1=P):
            nc.vector.scalar_tensor_tensor(
                g_rounded[i][a][:].rearrange("p (q t) -> p q t", t=PACK)[:, q0:q1, :],
                g_picked[i][a][:].rearrange("p (q t) -> p q t", t=PACK)[:, q0:q1, :],
                cp_sb[:, i : i + 1],
                rb_rows[a][:].rearrange("p t q -> p q t")[:, q0:q1, :],
                ALU.min, ALU.mult,
            )

        def turn_g(i, a):
            bank = psum.tile([P, PACK, P], F32, name="bank", tag=f"turn{3 - 2 * i - a}")
            words = g_rounded[i][a][:].bitcast(F32)
            for u in range(2):
                nc.tensor.transpose(bank[:, u, :], words[:, u : J_PASS // 2 : 2], ident[:])
            turned["g", i, a] = bank

        def group_g(i, a):
            nc.scalar.copy(
                g_grouped[i, a].bitcast(F32).rearrange("p (n u) -> p n u", u=2),
                turned["g", i, a][:, 0:2, :].rearrange("p u n -> p n u"),
            )

        def quantize_g(codes, scales, grouped):
            nc.vector.quantize_mx(out=codes.bitcast(E5M2X4), scales=scales, in_=grouped)

        def multiply(acc, i, h, a):
            nc.tensor.matmul_mx(
                out=acc[:],
                lhsT=x_codes[i][:, a, :].bitcast(E4M3X4),
                lhsT_scale=x_scales[i][:, a, :],
                rhs=g_codes[h][:, a, :].bitcast(E5M2X4),
                rhs_scale=g_scales[h][:, a, :],
                start=(a == 0),
                stop=(a == PASSES - 1),
            )

        accs = {}
        for i in range(2):
            accs[i, 0] = psum.tile([P, P], F32, name="acc", tag=f"acc{i}")

        gather_x("vector", 0, 0, 256)
        gather_x("scalar", 0, 256, 512)
        gather_x("scalar", 0, 512, 1024)
        diff_x(0, 0)
        diff_x(0, 1)
        gather_x("vector", 1, 0, 256)
        gather_x("scalar", 1, 256, 512)
        gather_x("scalar", 1, 512, 1024)
        weigh_x(0, 0)
        diff_x(1, 0)
        diff_x(1, 1)
        weigh_x(0, 1)
        gather_g("scalar", 0, 0, 512)
        gather_g("scalar", 0, 512, 768)
        gather_g("vector", 0, 768, 1024)
        gather_g("scalar", 1, 0, 512)
        gather_g("scalar", 1, 512, 768)
        gather_g("scalar", 1, 768, 1024)
        bound_g(0, 0)
        bound_g(0, 1)
        x_grouped[1] = held.tile([P, PASSES, P, PACK], BF16, name="x_grouped1", tag="g_picked00", align_bytes=64)
        weigh_x(1, 0)
        weigh_x(1, 1)
        bound_g(1, 0)
        bound_g(1, 1, 0, P // 2)
        bound_g(1, 1, P // 2, P)
        first = held.tile([P, J], BF16, name="g_grouped0", tag="g_picked10", align_bytes=64)
        for a in range(PASSES):
            g_grouped[0, a] = first[:, a * J_PASS : (a + 1) * J_PASS]
            g_grouped[1, a] = held.tile([P, J_PASS], BF16, name=f"g_grouped1{a}", align_bytes=64)[:]
        for i in range(2):
            for a in range(PASSES):
                turn_g(i, a)
                group_g(i, a)
        both = held.tile([P, 2, PASSES, P], U32, name="x_codes", tag="g_picked11", align_bytes=64)
        for i in range(2):
            x_codes[i] = both[:, i, :, :]
            accs[i, 1] = psum.tile([P, P], F32, name="acc", tag=f"turn{3 - i}")
        quantize_x(0)
        quantize_g(g_codes[0][:].rearrange("p a n -> p (a n)"), g_scales[0][:].rearrange("p a n -> p (a n)"), first[:])
        quantize_x(1)
        for a in range(PASSES):
            quantize_g(g_codes[1][:, a, :], g_scales[1][:, a, :], g_grouped[1, a])
        for i in range(2):
            for a in range(PASSES):
                multiply(accs[i, 0], i, 0, a)
        for a in range(PASSES):
            for i in range(2):
                multiply(accs[i, 1], i, 1, a)
        for i in range(2):
            nc.scalar.copy(w_sb[i][:, 0:P], accs[i, 0][:])
        nc.vector.tensor_copy(w_sb[0][:, P : 2 * P], accs[0, 1][:])
        nc.scalar.copy(w_sb[1][:, P : 2 * P], accs[1, 1][:])

        nc.vector.tensor_copy(w_picked[:, 0:E], w_sb[0][:].indirect(list_w[:]))
        nc.scalar.activation(w_picked[:, E : 2 * E], w_sb[1][:].indirect(list_w[:]), COPY)
        nc.vector.scalar_tensor_tensor(result[:], w_picked[:], 0.04, old_sb[:], ALU.mult, ALU.add)
        nc.sync.dma_start(out.rearrange("(p i) e -> p (i e)", i=2), result[:])
